import numpy as np
import ml_dtypes


def mxq(x, axis, fmt="e4m3"):
    dtype, down = {"e4m3": (ml_dtypes.float8_e4m3fn, 7), "e5m2": (ml_dtypes.float8_e5m2, 14)}[fmt]
    v = np.moveaxis(np.asarray(x, np.float32).astype(ml_dtypes.bfloat16).astype(np.float64), axis, -1)
    blocks = v.reshape(v.shape[:-1] + (-1, 32))
    amax = np.abs(blocks).max(-1, keepdims=True)
    byte = np.maximum(np.where(amax > 0, np.frexp(amax)[1] - 1 + 127, 0) - down, 1)
    scale = np.exp2(byte - 127.0)
    codes = (blocks / scale).astype(np.float32).astype(dtype).astype(np.float64)
    return np.moveaxis((codes * scale).reshape(v.shape), -1, axis)


WIDE = False


def mx_kscale(k):
    if not WIDE:
        return np.ones(k)
    levels = np.array([10, -10, 5, -5, 0])
    if k % 512:
        return np.exp2(np.random.permutation(np.resize(levels, k // 32))).repeat(32)
    a = np.empty((k // 512, 16))
    for p in range(k // 512):
        a[p, :8] = np.random.permutation(np.resize(levels, 8))
        for g in range(8):
            far = levels[np.abs(levels - a[p, g]) >= 10]
            a[p, g + 8] = far[np.random.randint(len(far))]
    return np.exp2(a.ravel()).repeat(32)


def f64(x):
    return np.asarray(x).astype(np.float64)


def striped(idx):
    return np.tile(idx.reshape(-1, 16).T, (8, 1)).astype(np.uint16)


def unstriped(offs):
    return offs[:16].T.reshape(-1).astype(np.int64)


E2M1 = np.array([0.0, 0.5, 1.0, 1.5, 2.0, 3.0, 4.0, 6.0, -0.0, -0.5, -1.0, -1.5, -2.0, -3.0, -4.0, -6.0])


def pack_weight(w, fmt):
    k, n = w.shape
    w = f64(np.asarray(w, np.float32).astype(ml_dtypes.bfloat16)).reshape(k // 32, 32, n)
    amax = np.abs(w).max(1)
    if fmt == "e4m3":
        byte = np.frexp(amax)[1] - 1 + 127 - 7
    else:
        mant, ex = np.frexp(amax / 6.0)
        byte = np.where(mant > 0.5, ex, ex - 1) + 127
    byte = np.clip(np.where(amax > 0, byte, 1), 1, 254)
    scaled = (w * np.exp2(127.0 - byte)[:, None, :]).reshape(k, n).astype(np.float32)
    by_word = np.ascontiguousarray(scaled.reshape(k // 512, 128, 4, n).transpose(0, 1, 3, 2))
    if fmt == "e4m3":
        words = by_word.astype(ml_dtypes.float8_e4m3fn).view(np.uint8)
    else:
        c = by_word.astype(ml_dtypes.float4_e2m1fn).view(np.uint8) & 0xF
        words = (c[..., 0::2] | (c[..., 1::2] << 4)).reshape(k // 512, 128, 2 * n)
    return np.ascontiguousarray(words), np.ascontiguousarray(byte.astype(np.uint8).reshape(k // 512, 16, n))


def unpack_weight(words, scales, fmt):
    g, _, n = scales.shape
    words = np.ascontiguousarray(words).reshape(g, 128, n, -1)
    if fmt == "e4m3":
        vals = words.view(ml_dtypes.float8_e4m3fn).astype(np.float64)
    else:
        nib = np.empty((g, 128, n, 4), np.uint8)
        nib[..., 0::2] = words & 0xF
        nib[..., 1::2] = words >> 4
        vals = E2M1[nib]
    vals = vals * np.repeat(np.exp2(scales.astype(np.float64) - 127.0), 8, axis=1)[..., None]
    return vals.transpose(0, 1, 3, 2).reshape(g * 512, n)


def gelu(v):
    return 0.5 * v * (1.0 + np.tanh(np.sqrt(2.0 / np.pi) * (v + 0.044715 * v**3)))


K, H, N, T, S, T2, P = 1024, 1024, 512, 4096, 1024, 2048, 1024

def setup_inputs():
    n = np.random.standard_normal
    s = mx_kscale(K)[:, None]
    u = mx_kscale(H)[:, None]
    d = {}
    d["tab_words"], d["tab_scales"] = pack_weight(n((K, T)) * s, "e4m3")
    d["offs"] = striped(np.random.permutation(T)[:S])
    d["w1"] = (n((K, H)) / s / K ** 0.5).astype(np.float32)
    d["smoke0"] = n((H, S)).astype(np.float32)
    d["gain"] = (np.random.uniform(0.6, 1.4, H) * u[:, 0]).astype(np.float32)
    d["wgs"] = np.exp(0.3 * n((128, S))).astype(np.float32)
    d["page0"] = (n((H, T2)) * u).astype(np.float32)
    d["offs2"] = striped(np.random.permutation(T2)[:S])
    d["offs3"] = striped(np.random.permutation(T2)[:P])
    d["bar"] = ((0.4 + 0.6 * n(H)) * u[:, 0]).astype(np.float32)
    d["w4_words"], d["w4_scales"] = pack_weight(n((H, N)) / u / H ** 0.5, "e2m1")
    d["w5"] = (n((H, N)) / u / H ** 0.5).astype(np.float32)
    d["wgo"] = np.exp(0.3 * n((128, P))).astype(np.float32)
    d["page1"] = n((N, T2)).astype(np.float32)
    d["offs4"] = striped(np.random.permutation(T2)[:P])
    return d

def reference(tab_words, tab_scales, offs, w1, smoke0, gain, wgs, page0, offs2, offs3, bar, w4_words, w4_scales, w5, wgo, page1, offs4):
    v = unpack_weight(tab_words, tab_scales, "e4m3")[:, unstriped(offs)]
    dev = (mxq(f64(w1), 0, "e4m3").T @ v) - f64(smoke0)
    h = f64(gain)[:, None] * np.abs(dev)
    page = f64(page0).copy()
    page[:, unstriped(offs2)] = np.tile(f64(wgs), (H // 128, 1)) * h
    x = page[:, unstriped(offs3)]
    hi = mxq(np.maximum(x, f64(bar)[:, None]), 0, "e4m3")
    lo = mxq(np.minimum(x, f64(bar)[:, None]), 0, "e4m3")
    yhi = unpack_weight(w4_words, w4_scales, "e2m1").T @ hi
    ylo = mxq(f64(w5), 0, "e4m3").T @ lo
    y = yhi - ylo
    out = f64(page1).copy()
    out[:, unstriped(offs4)] = np.tile(f64(wgo), (N // 128, 1)) * y
    return out

@@ -1,0 +1,376 @@
+from contextlib import ExitStack
+
+import concourse.mybir as mybir
+from concourse.masks import make_identity
+
+K, H, N, T, S, T2, M = 1024, 1024, 512, 4096, 1024, 2048, 1024
+FLOPS = 2 * K * H * S + 2 * 2 * H * N * M
+
+F32 = mybir.dt.float32
+BF16 = mybir.dt.bfloat16
+I32 = mybir.dt.int32
+U32 = mybir.dt.uint32
+U16 = mybir.dt.uint16
+U8 = mybir.dt.uint8
+FP8X4 = mybir.dt.float8_e4m3fn_x4
+FP4X4 = mybir.dt.float4_e2m1fn_x4
+ALU = mybir.AluOpType
+ACT = mybir.ActivationFunctionType
+
+P = 128
+PACK = 4
+PASS = P * PACK
+HALF = 512
+LIST_HALF = HALF // 16
+STEPS = H // P
+
+
+def tile_list_kiln_vent_page_kernel(
+    tc, tab_words, tab_scales, offs, w1, smoke0, gain, wgs, page0, offs2, offs3, bar,
+    w4_words, w4_scales, w5, wgo, page1, offs4, out,
+):
+    nc = tc.nc
+    with ExitStack() as ctx:
+        lists = ctx.enter_context(tc.tile_pool(name="lists", bufs=1))
+        keep = ctx.enter_context(tc.tile_pool(name="keep", bufs=1))
+        ring = ctx.enter_context(tc.tile_pool(name="ring", bufs=2))
+        psum = ctx.enter_context(tc.psum_pool(name="psum", bufs=2))
+
+        def load_list(src, name):
+            tile = lists.tile([P, S // 16], U16, name=name)
+            nc.sync.dma_start(tile[:], src)
+            return tile
+
+        def list_half(tile, half):
+            return tile[:, half * LIST_HALF:(half + 1) * LIST_HALF]
+
+        def load_channel_vector(src, name):
+            tile = keep.tile([P, STEPS], F32, name=name)
+            nc.sync.dma_start(
+                tile[:].rearrange("p (a t) -> p a t", t=PACK),
+                src.rearrange("(a p t) -> p a t", p=P, t=PACK),
+            )
+            return tile
+
+        def dealt_rows(src, s):
+            a, t = divmod(s, PACK)
+            return src[a * PASS:(a + 1) * PASS, :].rearrange("(p t) c -> p t c", t=PACK)[:, t, :]
+
+        def big_tile(shape, name):
+            return ring.tile(shape, F32, name=name, tag="big", bufs=6)
+
+        def woven_tile(name, tag="woven", bufs=2):
+            return ring.tile([P, PACK * HALF], BF16, name=name, tag=tag, bufs=bufs, align_bytes=64)
+
+        def load_weight(src, kp, cols, name):
+            raw = big_tile([P, PACK, HALF], name)
+            rows = src[kp * PASS:(kp + 1) * PASS, cols]
+            nc.sync.dma_start(raw[:], rows.rearrange("(p j) c -> p j c", j=PACK))
+            return raw
+
+        def quantise(woven, codes, scales):
+            nc.vector.quantize_mx(out=codes.bitcast(FP8X4), scales=scales, in_=woven[:])
+
+        def mx_tiles(name, width=HALF):
+            codes = keep.tile([P, width], U32, name=name + "_codes", align_bytes=64)
+            scales = keep.tile([P, width], U8, name=name + "_scales", align_bytes=64)
+            return codes, scales
+
+        w1q = {}
+
+        def quantise_w1(a, kp, raw):
+            woven = woven_tile("w1_woven")
+            nc.scalar.activation(
+                woven[:].rearrange("p (t m j) -> p m j t", t=PACK, j=PACK),
+                raw[:].rearrange("p j (m t) -> p m j t", t=PACK),
+                ACT.Copy,
+            )
+            w1q[a, kp] = mx_tiles("w1_%d_%d" % (a, kp))
+            quantise(woven, w1q[a, kp][0][:], w1q[a, kp][1][:])
+
+        w5q = {}
+
+        def quantise_w5(a, raw):
+            woven = woven_tile("w5_woven")
+            nc.scalar.activation(
+                woven[:].rearrange("p (c i j) -> p c j i", i=4, j=PACK),
+                raw[:].rearrange("p j (c i) -> p c j i", i=4),
+                ACT.Copy,
+                scale=-1.0,
+            )
+            w5q[a] = mx_tiles("w5_%d" % a)
+            quantise(woven, w5q[a][0][:], w5q[a][1][:])
+
+        smoke = {}
+        page = {}
+        wgs_dealt = {}
+
+        def load_smoke(s):
+            smoke[s] = ring.tile([P, S], F32, name="smoke", tag="smoke", bufs=3)
+            nc.sync.dma_start(smoke[s][:], dealt_rows(smoke0, s))
+
+        def load_page(s):
+            page[s] = big_tile([P, T2], "page")
+            nc.sync.dma_start(page[s][:], dealt_rows(page0, s))
+
+        def load_wgs(t):
+            wgs_dealt[t] = keep.tile([P, S], F32, name="wgs_%d" % t)
+            rows = wgs.rearrange("(m t) j -> m t j", t=PACK)[:, t, :]
+            for q in (0, 2, 1, 3):
+                nc.sync.dma_start(wgs_dealt[t][32 * q:32 * (q + 1), :], rows)
+
+        v_words = {}
+        v_scales = {}
+        with tc.tile_pool(name="table", bufs=1) as table:
+            tab_sc = table.tile([P, T], U8, name="tab_sc")
+            nc.vector.memset(tab_sc[:].bitcast(I32), 0)
+            def load_words(kp):
+                words = table.tile([P, T], I32, name="tab_%d" % kp)
+                nc.sync.dma_start(words[:], tab_words[kp].rearrange("p t i -> p (t i)").bitcast(I32))
+                return words
+
+            idx = load_list(offs, "idx")
+            w1_raw = [load_weight(w1, 0, slice(0, HALF), "w1_raw")]
+            gain_sb = load_channel_vector(gain, "gain_sb")
+            idx2 = load_list(offs2, "idx2")
+            w1_raw.append(load_weight(w1, 1, slice(0, HALF), "w1_raw"))
+            bar_sb = load_channel_vector(bar, "bar_sb")
+            tab = [load_words(0)]
+            idx3 = load_list(offs3, "idx3")
+            for q in range(4):
+                nc.sync.dma_start(
+                    tab_sc[32 * q:32 * q + 8, :].bitcast(I32),
+                    tab_scales[:, 4 * q:4 * q + 4, :].bitcast(I32),
+                )
+            tab.append(load_words(1))
+            ident = keep.tile([P, P], F32, name="ident")
+            make_identity(nc, ident[:])
+            w4_sc = keep.tile([P, 2, N], U8, name="w4_sc", align_bytes=64)
+            nc.vector.memset(w4_sc[:].bitcast(I32), 0)
+            load_smoke(0)
+            load_wgs(0)
+            load_page(0)
+            for kp in range(2):
+                quantise_w1(0, kp, w1_raw[kp])
+            for half in range(2):
+                v_scales[half] = keep.tile([P, HALF], U8, name="v_sc_%d" % half, align_bytes=64)
+                nc.vector.tensor_copy(v_scales[half][:], tab_sc[:].indirect(list_half(idx, half)))
+                for kp in range(2):
+                    v_words[kp, half] = keep.tile([P, HALF], U32, name="v_%d_%d" % (kp, half), align_bytes=64)
+                    nc.vector.tensor_copy(
+                        v_words[kp, half][:], tab[kp][:].bitcast(U32).indirect(list_half(idx, half))
+                    )
+        vent = ctx.enter_context(tc.tile_pool(name="vent", bufs=1))
+
+        h = {}
+
+        def make_h(s):
+            a, t = divmod(s, PACK)
+            if s in (4, 5, 7):
+                h[s] = ring.tile([P, S], F32, name="h", tag="h%d" % s, bufs=1, align_bytes=64)
+            else:
+                h[s] = ring.tile([P, S], F32, name="h", tag="h", bufs=2)
+            cols = slice(t * P, (t + 1) * P)
+            for half in range(2):
+                acc = psum.tile([P, HALF], F32, name="acc")
+                for kp in range(2):
+                    codes, scales = w1q[a, kp]
+                    nc.tensor.matmul_mx(
+                        out=acc[:],
+                        lhsT=codes[:, cols].bitcast(FP8X4),
+                        lhsT_scale=scales[:, cols],
+                        rhs=v_words[kp, half][:].bitcast(FP8X4),
+                        rhs_scale=v_scales[half][4 * kp:P, :],
+                        start=(kp == 0),
+                        stop=(kp == 1),
+                    )
+                if s == 0 and half == 0:
+                    diff = ring.tile([P, HALF], F32, name="diff", tag="negated")
+                    nc.vector.tensor_tensor(diff[:], acc[:], smoke[s][:, 0:HALF], ALU.subtract)
+                    size = ring.tile([P, HALF], F32, name="size", tag="abs_t")
+                    nc.vector.scalar_tensor_tensor(size[:], diff[:], -1.0, diff[:], ALU.mult, ALU.max)
+                    nc.vector.tensor_scalar(h[s][:, 0:HALF], size[:], gain_sb[:, s:s + 1], None, ALU.mult)
+                    continue
+                negated = ring.tile([P, HALF], F32, name="negated", tag="negated")
+                nc.scalar.activation(negated[:], acc[:], ACT.Copy, scale=-1.0)
+                diff_t = psum.tile([P, HALF], F32, name="diff_t")
+                blocks = HALF // P
+                for b in range(blocks):
+                    nc.tensor.matmul(
+                        diff_t[:, b * P:(b + 1) * P],
+                        smoke[s][:, half * HALF + b * P:half * HALF + (b + 1) * P],
+                        ident[:], start=(b == 0), stop=False, is_transpose=True,
+                    )
+                for b in range(blocks):
+                    nc.tensor.matmul(
+                        diff_t[:, b * P:(b + 1) * P],
+                        negated[:, b * P:(b + 1) * P],
+                        ident[:], start=False, stop=(b == blocks - 1), is_transpose=True,
+                    )
+                abs_t = ring.tile([P, HALF], F32, name="abs_t", tag="abs_t")
+                nc.scalar.activation(abs_t[:], diff_t[:], ACT.Abs)
+                back = psum.tile([P, HALF], F32, name="back")
+                for b in range(blocks):
+                    nc.tensor.transpose(back[:, b * P:(b + 1) * P], abs_t[:, b * P:(b + 1) * P], ident[:])
+                nc.scalar.activation(
+                    h[s][:, half * HALF:(half + 1) * HALF], back[:], ACT.Copy, scale=gain_sb[:, s:s + 1]
+                )
+
+        def scatter_page(s):
+            if s == 0:
+                for half in range(2):
+                    cols = slice(half * HALF, (half + 1) * HALF)
+                    nc.vector.tensor_tensor(
+                        page[s][:].indirect(list_half(idx2, half)), h[s][:, cols], wgs_dealt[0][:, cols], ALU.mult
+                    )
+            else:
+                nc.vector.tensor_tensor(page[s][:].indirect(idx2[:]), h[s][:], wgs_dealt[s % PACK][:], ALU.mult)
+
+        def split_at_bar(s, x, hi_plane, lo_plane):
+            nc.vector.tensor_scalar(hi_plane, x, bar_sb[:, s:s + 1], None, ALU.max)
+            nc.vector.tensor_scalar(lo_plane, x, bar_sb[:, s:s + 1], None, ALU.min)
+
+        def planes_tile(shape, name):
+            return ring.tile(shape, BF16, name=name, tag="planes", bufs=3)
+
+        def weave(planes, woven):
+            nc.scalar.copy(
+                woven[:].rearrange("p (c i t) -> p c t i", i=4, t=PACK),
+                planes.rearrange("p t (c i) -> p c t i", i=4),
+            )
+
+        def gather_half(s, half, x):
+            nc.vector.tensor_copy(x[:], page[s][:].indirect(list_half(idx3, half)))
+
+        def load_second_stage_weights():
+            w4 = keep.tile([P, 2, 2 * N], U8, name="w4", align_bytes=64)
+            nc.sync.dma_start(w4[:].bitcast(I32), w4_words.rearrange("a p c -> p a c").bitcast(I32))
+            for q in range(4):
+                nc.sync.dma_start(
+                    w4_sc[32 * q:32 * q + 4, :, :].bitcast(I32),
+                    w4_scales[:, 4 * q:4 * q + 4, :].rearrange("a r n -> r a n").bitcast(I32),
+                )
+            return w4
+
+        make_h(0)
+        load_smoke(1)
+        load_wgs(1)
+        load_page(1)
+        hi0 = planes_tile([P, PACK, M], "hi0")
+        lo0 = planes_tile([P, PACK, M], "lo0")
+        for s in range(PACK):
+            if s == 0:
+                load_smoke(2)
+                load_wgs(2)
+                load_page(2)
+            if s == 1:
+                load_smoke(3)
+                load_wgs(3)
+                w1_raw = [load_weight(w1, kp, slice(HALF, 2 * HALF), "w1_raw") for kp in range(2)]
+                load_smoke(4)
+                load_smoke(5)
+                load_page(3)
+                for kp in range(2):
+                    quantise_w1(1, kp, w1_raw[kp])
+            if s == 2:
+                load_page(4)
+                load_smoke(6)
+            if s == 3:
+                load_page(5)
+                load_smoke(7)
+            make_h(s + 1)
+            scatter_page(s)
+            x = ring.tile([P, M], F32, name="x", tag="x", bufs=2)
+            nc.vector.tensor_copy(x[:], page[s][:].indirect(idx3[:]))
+            split_at_bar(s, x[:], hi0[:, s, :], lo0[:, s, :])
+
+        w5_raw = [load_weight(w5, a, slice(0, N), "w5_raw") for a in range(2)]
+        w4 = load_second_stage_weights()
+        idx4 = load_list(offs4, "idx4")
+        load_page(6)
+        load_page(7)
+        wgo_sb = vent.tile([P, M], F32, name="wgo_sb")
+        nc.sync.dma_start(wgo_sb[:], wgo)
+        vent_page = []
+        for n in range(N // P):
+            tile = vent.tile([P, T2], F32, name="vent_%d" % n)
+            nc.sync.dma_start(tile[:], page1[n * P:(n + 1) * P, :])
+            vent_page.append(tile)
+
+        q = {}
+        planes = {0: planes_tile([P, 2, PACK, HALF], "planes_0")}
+        for s in range(PACK, STEPS):
+            t = s - PACK
+            if s + 1 < STEPS:
+                make_h(s + 1)
+            scatter_page(s)
+            if s in (4, 5):
+                kind, src = (("hi", hi0), ("lo", lo0))[s - 4]
+                codes = ring.tile([P, M], U32, name="codes0", tag="h%d" % s, bufs=1, align_bytes=64)
+                scales = keep.tile([P, M], U8, name=kind + "0_scales", align_bytes=64)
+                for half in range(2):
+                    cols = slice(half * HALF, (half + 1) * HALF)
+                    woven = woven_tile("woven")
+                    weave(src[:, :, cols], woven)
+                    quantise(woven, codes[:, cols], scales[:, cols])
+                    q[kind, 0, half] = (codes[:, cols], scales[:, cols])
+            if s in (5, 6):
+                quantise_w5(s - 5, w5_raw[s - 5])
+            if s == 7:
+                x = ring.tile([P, HALF], F32, name="x", tag="xl", bufs=1)
+            else:
+                x = ring.tile([P, HALF], F32, name="x", tag="x", bufs=2)
+            gather_half(s, 0, x)
+            split_at_bar(s, x[:], planes[0][:, 0, t, :], planes[0][:, 1, t, :])
+
+        def quantise_pass1(half, tags):
+            for i, kind in enumerate(("hi", "lo")):
+                woven = woven_tile("woven", *tags[i])
+                weave(planes[half][:, i, :, :], woven)
+                codes, scales = mx_tiles("%s1_%d" % (kind, half))
+                quantise(woven, codes[:], scales[:])
+                q[kind, 1, half] = (codes[:], scales[:])
+
+        def second_stage(n, half, tag, bufs):
+            acc = psum.tile([P, HALF], F32, name="acc2")
+            cols = slice(n * P, (n + 1) * P)
+            for a in range(2):
+                nc.tensor.matmul_mx(
+                    out=acc[:],
+                    lhsT=w4[:, a, 2 * n * P:2 * (n + 1) * P].bitcast(FP4X4),
+                    lhsT_scale=w4_sc[:, a, cols],
+                    rhs=q["hi", a, half][0].bitcast(FP8X4),
+                    rhs_scale=q["hi", a, half][1],
+                    start=(a == 0), stop=False,
+                )
+                nc.tensor.matmul_mx(
+                    out=acc[:],
+                    lhsT=w5q[a][0][:, cols].bitcast(FP8X4),
+                    lhsT_scale=w5q[a][1][:, cols],
+                    rhs=q["lo", a, half][0].bitcast(FP8X4),
+                    rhs_scale=q["lo", a, half][1],
+                    start=False, stop=(a == 1),
+                )
+            y = ring.tile([P, HALF], F32, name="y", tag=tag, bufs=bufs, align_bytes=64)
+            nc.scalar.copy(y[:], acc[:])
+            nc.vector.tensor_tensor(
+                vent_page[n][:].indirect(list_half(idx4, half)), y[:],
+                wgo_sb[:, half * HALF:(half + 1) * HALF], ALU.mult,
+            )
+
+        quantise_pass1(0, (("woven", 2), ("g2", 1)))
+        planes[1] = planes_tile([P, 2, PACK, HALF], "planes_1")
+        for s, tag in ((4, "h7"), (5, "xl"), (6, "h7"), (7, "g2")):
+            if tag == "xl":
+                x = ring.tile([P, HALF], F32, name="x", tag=tag, bufs=1)
+            else:
+                x = ring.tile([P, HALF], F32, name="x", tag=tag, bufs=1, align_bytes=64)
+            gather_half(s, 1, x)
+            split_at_bar(s, x[:], planes[1][:, 0, s - PACK, :], planes[1][:, 1, s - PACK, :])
+        for n in range(3):
+            second_stage(n, 0, "y", 2)
+        quantise_pass1(1, (("g4", 1), ("woven", 2)))
+        second_stage(3, 0, "g4", 1)
+        for n in range(N // P):
+            second_stage(n, 1, "y", 2)
+            nc.sync.dma_start(out[n * P:(n + 1) * P, :], vent_page[n][:])

@@ -23,6 +23,7 @@ PASS = P * PACK
 HALF = 512
 LIST_HALF = HALF // 16
 STEPS = H // P
+F32_MAX = (2.0 - 2.0 ** -23) * 2.0 ** 127
 
 
 def tile_list_kiln_vent_page_kernel(
@@ -59,7 +60,7 @@ def tile_list_kiln_vent_page_kernel(
         def big_tile(shape, name):
             return ring.tile(shape, F32, name=name, tag="big", bufs=6)
 
-        def woven_tile(name, tag="woven", bufs=2):
+        def woven_tile(name, tag="woven", bufs=4):
             return ring.tile([P, PACK * HALF], BF16, name=name, tag=tag, bufs=bufs, align_bytes=64)
 
         def load_weight(src, kp, cols, name):
@@ -80,44 +81,43 @@ def tile_list_kiln_vent_page_kernel(
 
         def quantise_w1(a, kp, raw):
             woven = woven_tile("w1_woven")
-            nc.scalar.activation(
-                woven[:].rearrange("p (t m j) -> p m j t", t=PACK, j=PACK),
-                raw[:].rearrange("p j (m t) -> p m j t", t=PACK),
-                ACT.Copy,
+            copy = nc.vector.tensor_copy if a == 0 else nc.scalar.copy
+            copy(
+                woven[:].rearrange("p (t m j) -> p m t j", t=PACK, j=PACK),
+                raw[:].rearrange("p j (m t) -> p m t j", t=PACK),
             )
             w1q[a, kp] = mx_tiles("w1_%d_%d" % (a, kp))
             quantise(woven, w1q[a, kp][0][:], w1q[a, kp][1][:])
 
-        w5q = {}
-
-        def quantise_w5(a, raw):
-            woven = woven_tile("w5_woven")
+        def weave_w5(a, raw):
+            woven = woven_tile("w5_woven", ("g2", "g4")[a], 1)
             nc.scalar.activation(
                 woven[:].rearrange("p (c i j) -> p c j i", i=4, j=PACK),
                 raw[:].rearrange("p j (c i) -> p c j i", i=4),
                 ACT.Copy,
                 scale=-1.0,
             )
-            w5q[a] = mx_tiles("w5_%d" % a)
-            quantise(woven, w5q[a][0][:], w5q[a][1][:])
+            return woven
 
         smoke = {}
         page = {}
         wgs_dealt = {}
 
-        def load_smoke(s):
-            smoke[s] = ring.tile([P, S], F32, name="smoke", tag="smoke", bufs=3)
-            nc.sync.dma_start(smoke[s][:], dealt_rows(smoke0, s))
+        def load_smoke(s, cols=slice(0, S)):
+            if s not in smoke:
+                smoke[s] = ring.tile([P, S], F32, name="smoke", tag="smoke", bufs=3)
+            nc.sync.dma_start(smoke[s][:, cols], dealt_rows(smoke0, s)[:, cols])
 
         def load_page(s):
             page[s] = big_tile([P, T2], "page")
             nc.sync.dma_start(page[s][:], dealt_rows(page0, s))
 
-        def load_wgs(t):
-            wgs_dealt[t] = keep.tile([P, S], F32, name="wgs_%d" % t)
-            rows = wgs.rearrange("(m t) j -> m t j", t=PACK)[:, t, :]
+        def load_wgs(t, cols=slice(0, S)):
+            if t not in wgs_dealt:
+                wgs_dealt[t] = ring.tile([P, S], F32, name="wgs", tag="wgs%d" % t, bufs=1, align_bytes=64)
+            rows = wgs.rearrange("(m t) j -> m t j", t=PACK)[:, t, cols]
             for q in (0, 2, 1, 3):
-                nc.sync.dma_start(wgs_dealt[t][32 * q:32 * (q + 1), :], rows)
+                nc.sync.dma_start(wgs_dealt[t][32 * q:32 * (q + 1), cols], rows)
 
         v_words = {}
         v_scales = {}
@@ -145,6 +145,9 @@ def tile_list_kiln_vent_page_kernel(
             tab.append(load_words(1))
             ident = keep.tile([P, P], F32, name="ident")
             make_identity(nc, ident[:])
+            limits = keep.tile([P, 2], F32, name="limits")
+            nc.vector.memset(limits[:, 0:1], F32_MAX)
+            nc.vector.memset(limits[:, 1:2], -F32_MAX)
             w4_sc = keep.tile([P, 2, N], U8, name="w4_sc", align_bytes=64)
             nc.vector.memset(w4_sc[:].bitcast(I32), 0)
             load_smoke(0)
@@ -166,10 +169,7 @@ def tile_list_kiln_vent_page_kernel(
 
         def make_h(s):
             a, t = divmod(s, PACK)
-            if s in (4, 5, 7):
-                h[s] = ring.tile([P, S], F32, name="h", tag="h%d" % s, bufs=1, align_bytes=64)
-            else:
-                h[s] = ring.tile([P, S], F32, name="h", tag="h", bufs=2)
+            h[s] = ring.tile([P, S], F32, name="h", tag="h", bufs=3)
             cols = slice(t * P, (t + 1) * P)
             for half in range(2):
                 acc = psum.tile([P, HALF], F32, name="acc")
@@ -230,6 +230,10 @@ def tile_list_kiln_vent_page_kernel(
             nc.vector.tensor_scalar(hi_plane, x, bar_sb[:, s:s + 1], None, ALU.max)
             nc.vector.tensor_scalar(lo_plane, x, bar_sb[:, s:s + 1], None, ALU.min)
 
+        def split_at_bar_beside(s, x, hi_plane, lo_plane):
+            nc.gpsimd.tensor_scalar(hi_plane, x, limits[:, 0:1], bar_sb[:, s:s + 1], ALU.min, ALU.max)
+            nc.gpsimd.tensor_scalar(lo_plane, x, bar_sb[:, s:s + 1], limits[:, 1:2], ALU.min, ALU.max)
+
         def planes_tile(shape, name):
             return ring.tile(shape, BF16, name=name, tag="planes", bufs=3)
 
@@ -262,29 +266,35 @@ def tile_list_kiln_vent_page_kernel(
             if s == 0:
                 load_smoke(2)
                 load_wgs(2)
+                w1_raw = [load_weight(w1, kp, slice(HALF, 2 * HALF), "w1_raw") for kp in range(2)]
                 load_page(2)
             if s == 1:
                 load_smoke(3)
                 load_wgs(3)
-                w1_raw = [load_weight(w1, kp, slice(HALF, 2 * HALF), "w1_raw") for kp in range(2)]
                 load_smoke(4)
                 load_smoke(5)
+                w5_raw = [load_weight(w5, a, slice(0, N), "w5_raw") for a in range(2)]
+                load_smoke(6)
                 load_page(3)
                 for kp in range(2):
                     quantise_w1(1, kp, w1_raw[kp])
             if s == 2:
+                load_smoke(7)
                 load_page(4)
-                load_smoke(6)
             if s == 3:
                 load_page(5)
-                load_smoke(7)
             make_h(s + 1)
+            if s == 3:
+                w5_woven = [weave_w5(a, w5_raw[a]) for a in range(2)]
             scatter_page(s)
             x = ring.tile([P, M], F32, name="x", tag="x", bufs=2)
             nc.vector.tensor_copy(x[:], page[s][:].indirect(idx3[:]))
-            split_at_bar(s, x[:], hi0[:, s, :], lo0[:, s, :])
+            if s < 3:
+                split_at_bar_beside(s, x[:], hi0[:, s, :], lo0[:, s, :])
+            else:
+                nc.gpsimd.tensor_scalar(hi0[:, s, :], x[:], limits[:, 0:1], bar_sb[:, s:s + 1], ALU.min, ALU.max)
+                nc.vector.tensor_scalar(lo0[:, s, :], x[:], bar_sb[:, s:s + 1], None, ALU.min)
 
-        w5_raw = [load_weight(w5, a, slice(0, N), "w5_raw") for a in range(2)]
         w4 = load_second_stage_weights()
         idx4 = load_list(offs4, "idx4")
         load_page(6)
@@ -304,9 +314,21 @@ def tile_list_kiln_vent_page_kernel(
             if s + 1 < STEPS:
                 make_h(s + 1)
             scatter_page(s)
-            if s in (4, 5):
-                kind, src = (("hi", hi0), ("lo", lo0))[s - 4]
-                codes = ring.tile([P, M], U32, name="codes0", tag="h%d" % s, bufs=1, align_bytes=64)
+            if s == 7:
+                x = ring.tile([P, HALF], F32, name="x", tag="xl", bufs=1)
+            else:
+                x = ring.tile([P, HALF], F32, name="x", tag="x", bufs=2)
+            gather_half(s, 0, x)
+            split = split_at_bar_beside if s < 6 else split_at_bar
+            split(s, x[:], planes[0][:, 0, t, :], planes[0][:, 1, t, :])
+            if s == 4:
+                w5_codes = ring.tile([P, 2, N], U32, name="w5_codes", tag="wgs0", bufs=1, align_bytes=64)
+                w5_scales = keep.tile([P, 2, N], U8, name="w5_scales", align_bytes=64)
+                for a in range(2):
+                    quantise(w5_woven[a], w5_codes[:, a, :], w5_scales[:, a, :])
+            if s in (5, 6):
+                kind, src = (("hi", hi0), ("lo", lo0))[s - 5]
+                codes = ring.tile([P, M], U32, name="codes0", tag="wgs%d" % t, bufs=1, align_bytes=64)
                 scales = keep.tile([P, M], U8, name=kind + "0_scales", align_bytes=64)
                 for half in range(2):
                     cols = slice(half * HALF, (half + 1) * HALF)
@@ -314,14 +336,6 @@ def tile_list_kiln_vent_page_kernel(
                     weave(src[:, :, cols], woven)
                     quantise(woven, codes[:, cols], scales[:, cols])
                     q[kind, 0, half] = (codes[:, cols], scales[:, cols])
-            if s in (5, 6):
-                quantise_w5(s - 5, w5_raw[s - 5])
-            if s == 7:
-                x = ring.tile([P, HALF], F32, name="x", tag="xl", bufs=1)
-            else:
-                x = ring.tile([P, HALF], F32, name="x", tag="x", bufs=2)
-            gather_half(s, 0, x)
-            split_at_bar(s, x[:], planes[0][:, 0, t, :], planes[0][:, 1, t, :])
 
         def quantise_pass1(half, tags):
             for i, kind in enumerate(("hi", "lo")):
@@ -345,8 +359,8 @@ def tile_list_kiln_vent_page_kernel(
                 )
                 nc.tensor.matmul_mx(
                     out=acc[:],
-                    lhsT=w5q[a][0][:, cols].bitcast(FP8X4),
-                    lhsT_scale=w5q[a][1][:, cols],
+                    lhsT=w5_codes[:, a, cols].bitcast(FP8X4),
+                    lhsT_scale=w5_scales[:, a, cols],
                     rhs=q["lo", a, half][0].bitcast(FP8X4),
                     rhs_scale=q["lo", a, half][1],
                     start=False, stop=(a == 1),
@@ -358,9 +372,9 @@ def tile_list_kiln_vent_page_kernel(
                 wgo_sb[:, half * HALF:(half + 1) * HALF], ALU.mult,
             )
 
-        quantise_pass1(0, (("woven", 2), ("g2", 1)))
+        quantise_pass1(0, (("woven", 4), ("g2", 1)))
         planes[1] = planes_tile([P, 2, PACK, HALF], "planes_1")
-        for s, tag in ((4, "h7"), (5, "xl"), (6, "h7"), (7, "g2")):
+        for s, tag in ((4, "wgs3"), (5, "xl"), (6, "wgs3"), (7, "g2")):
             if tag == "xl":
                 x = ring.tile([P, HALF], F32, name="x", tag=tag, bufs=1)
             else:
@@ -369,7 +383,7 @@ def tile_list_kiln_vent_page_kernel(
             split_at_bar(s, x[:], planes[1][:, 0, s - PACK, :], planes[1][:, 1, s - PACK, :])
         for n in range(3):
             second_stage(n, 0, "y", 2)
-        quantise_pass1(1, (("g4", 1), ("woven", 2)))
+        quantise_pass1(1, (("g4", 1), ("woven", 4)))
         second_stage(3, 0, "g4", 1)
         for n in range(N // P):
             second_stage(n, 1, "y", 2)

@@ -145,14 +145,14 @@ def tile_list_kiln_vent_page_kernel(
             tab.append(load_words(1))
             ident = keep.tile([P, P], F32, name="ident")
             make_identity(nc, ident[:])
-            limits = keep.tile([P, 2], F32, name="limits")
+            limits = keep.tile([P, 1], F32, name="limits")
             nc.vector.memset(limits[:, 0:1], F32_MAX)
-            nc.vector.memset(limits[:, 1:2], -F32_MAX)
             w4_sc = keep.tile([P, 2, N], U8, name="w4_sc", align_bytes=64)
             nc.vector.memset(w4_sc[:].bitcast(I32), 0)
             load_smoke(0)
-            load_wgs(0)
+            load_wgs(0, slice(0, HALF))
             load_page(0)
+            load_wgs(0, slice(HALF, S))
             for kp in range(2):
                 quantise_w1(0, kp, w1_raw[kp])
             for half in range(2):
@@ -232,7 +232,9 @@ def tile_list_kiln_vent_page_kernel(
 
         def split_at_bar_beside(s, x, hi_plane, lo_plane):
             nc.gpsimd.tensor_scalar(hi_plane, x, limits[:, 0:1], bar_sb[:, s:s + 1], ALU.min, ALU.max)
-            nc.gpsimd.tensor_scalar(lo_plane, x, bar_sb[:, s:s + 1], limits[:, 1:2], ALU.min, ALU.max)
+            short = ring.tile([P, x.shape[1]], F32, name="short", tag="abs_t")
+            nc.scalar.activation(short[:], x, ACT.Relu, bias=bar_sb[:, s:s + 1], scale=-1.0)
+            nc.scalar.activation(lo_plane, short[:], ACT.Identity, bias=bar_sb[:, s:s + 1], scale=-1.0)
 
         def planes_tile(shape, name):
             return ring.tile(shape, BF16, name=name, tag="planes", bufs=3)
@@ -260,6 +262,7 @@ def tile_list_kiln_vent_page_kernel(
         load_smoke(1)
         load_wgs(1)
         load_page(1)
+        make_h(1)
         hi0 = planes_tile([P, PACK, M], "hi0")
         lo0 = planes_tile([P, PACK, M], "lo0")
         for s in range(PACK):
@@ -283,17 +286,13 @@ def tile_list_kiln_vent_page_kernel(
                 load_page(4)
             if s == 3:
                 load_page(5)
-            make_h(s + 1)
+            make_h(s + 2)
             if s == 3:
                 w5_woven = [weave_w5(a, w5_raw[a]) for a in range(2)]
             scatter_page(s)
             x = ring.tile([P, M], F32, name="x", tag="x", bufs=2)
             nc.vector.tensor_copy(x[:], page[s][:].indirect(idx3[:]))
-            if s < 3:
-                split_at_bar_beside(s, x[:], hi0[:, s, :], lo0[:, s, :])
-            else:
-                nc.gpsimd.tensor_scalar(hi0[:, s, :], x[:], limits[:, 0:1], bar_sb[:, s:s + 1], ALU.min, ALU.max)
-                nc.vector.tensor_scalar(lo0[:, s, :], x[:], bar_sb[:, s:s + 1], None, ALU.min)
+            split_at_bar_beside(s, x[:], hi0[:, s, :], lo0[:, s, :])
 
         w4 = load_second_stage_weights()
         idx4 = load_list(offs4, "idx4")
@@ -311,15 +310,15 @@ def tile_list_kiln_vent_page_kernel(
         planes = {0: planes_tile([P, 2, PACK, HALF], "planes_0")}
         for s in range(PACK, STEPS):
             t = s - PACK
-            if s + 1 < STEPS:
-                make_h(s + 1)
+            if s + 2 < STEPS:
+                make_h(s + 2)
             scatter_page(s)
             if s == 7:
                 x = ring.tile([P, HALF], F32, name="x", tag="xl", bufs=1)
             else:
                 x = ring.tile([P, HALF], F32, name="x", tag="x", bufs=2)
             gather_half(s, 0, x)
-            split = split_at_bar_beside if s < 6 else split_at_bar
+            split = split_at_bar_beside if s < 7 else split_at_bar
             split(s, x[:], planes[0][:, 0, t, :], planes[0][:, 1, t, :])
             if s == 4:
                 w5_codes = ring.tile([P, 2, N], U32, name="w5_codes", tag="wgs0", bufs=1, align_bytes=64)

@@ -276,7 +276,6 @@ def tile_list_kiln_vent_page_kernel(
                 load_wgs(3)
                 load_smoke(4)
                 load_smoke(5)
-                w5_raw = [load_weight(w5, a, slice(0, N), "w5_raw") for a in range(2)]
                 load_smoke(6)
                 load_page(3)
                 for kp in range(2):
@@ -286,9 +285,8 @@ def tile_list_kiln_vent_page_kernel(
                 load_page(4)
             if s == 3:
                 load_page(5)
+                w5_raw = [load_weight(w5, a, slice(0, N), "w5_raw") for a in range(2)]
             make_h(s + 2)
-            if s == 3:
-                w5_woven = [weave_w5(a, w5_raw[a]) for a in range(2)]
             scatter_page(s)
             x = ring.tile([P, M], F32, name="x", tag="x", bufs=2)
             nc.vector.tensor_copy(x[:], page[s][:].indirect(idx3[:]))
@@ -314,19 +312,28 @@ def tile_list_kiln_vent_page_kernel(
                 make_h(s + 2)
             scatter_page(s)
             if s == 7:
-                x = ring.tile([P, HALF], F32, name="x", tag="xl", bufs=1)
+                quarters = [ring.tile([P, HALF // 2], F32, name="x", tag=tag, bufs=1) for tag in ("xa", "xb")]
+                for i in range(2):
+                    offsets = idx3[:, i * LIST_HALF // 2:(i + 1) * LIST_HALF // 2]
+                    nc.vector.tensor_copy(quarters[i][:], page[s][:].indirect(offsets))
+                for kind, op in enumerate((ALU.max, ALU.min)):
+                    for i in range(2):
+                        cols = slice(i * HALF // 2, (i + 1) * HALF // 2)
+                        nc.vector.tensor_scalar(
+                            planes[0][:, kind, t, cols], quarters[i][:], bar_sb[:, s:s + 1], None, op
+                        )
             else:
                 x = ring.tile([P, HALF], F32, name="x", tag="x", bufs=2)
-            gather_half(s, 0, x)
-            split = split_at_bar_beside if s < 7 else split_at_bar
-            split(s, x[:], planes[0][:, 0, t, :], planes[0][:, 1, t, :])
-            if s == 4:
-                w5_codes = ring.tile([P, 2, N], U32, name="w5_codes", tag="wgs0", bufs=1, align_bytes=64)
+                gather_half(s, 0, x)
+                split_at_bar_beside(s, x[:], planes[0][:, 0, t, :], planes[0][:, 1, t, :])
+            if s == 6:
+                w5_woven = [weave_w5(a, w5_raw[a]) for a in range(2)]
+                w5_codes = ring.tile([P, 2, N], U32, name="w5_codes", tag="wgs2", bufs=1, align_bytes=64)
                 w5_scales = keep.tile([P, 2, N], U8, name="w5_scales", align_bytes=64)
                 for a in range(2):
                     quantise(w5_woven[a], w5_codes[:, a, :], w5_scales[:, a, :])
-            if s in (5, 6):
-                kind, src = (("hi", hi0), ("lo", lo0))[s - 5]
+            if s in (4, 5):
+                kind, src = (("lo", lo0), ("hi", hi0))[s - 4]
                 codes = ring.tile([P, M], U32, name="codes0", tag="wgs%d" % t, bufs=1, align_bytes=64)
                 scales = keep.tile([P, M], U8, name=kind + "0_scales", align_bytes=64)
                 for half in range(2):
@@ -373,13 +380,19 @@ def tile_list_kiln_vent_page_kernel(
 
         quantise_pass1(0, (("woven", 4), ("g2", 1)))
         planes[1] = planes_tile([P, 2, PACK, HALF], "planes_1")
-        for s, tag in ((4, "wgs3"), (5, "xl"), (6, "wgs3"), (7, "g2")):
-            if tag == "xl":
+        for s, tag in ((4, "xa"), (5, "xb"), (6, "xa"), (7, "g2")):
+            if tag != "g2":
                 x = ring.tile([P, HALF], F32, name="x", tag=tag, bufs=1)
             else:
                 x = ring.tile([P, HALF], F32, name="x", tag=tag, bufs=1, align_bytes=64)
             gather_half(s, 1, x)
-            split_at_bar(s, x[:], planes[1][:, 0, s - PACK, :], planes[1][:, 1, s - PACK, :])
+            if s < 6:
+                nc.gpsimd.tensor_scalar(
+                    planes[1][:, 0, s - PACK, :], x[:], limits[:, 0:1], bar_sb[:, s:s + 1], ALU.min, ALU.max
+                )
+                nc.vector.tensor_scalar(planes[1][:, 1, s - PACK, :], x[:], bar_sb[:, s:s + 1], None, ALU.min)
+            else:
+                split_at_bar(s, x[:], planes[1][:, 0, s - PACK, :], planes[1][:, 1, s - PACK, :])
         for n in range(3):
             second_stage(n, 0, "y", 2)
         quantise_pass1(1, (("g4", 1), ("woven", 4)))

from contextlib import ExitStack

import concourse.mybir as mybir
from concourse.masks import make_identity

K, H, N, T, S, T2, M = 1024, 1024, 512, 4096, 1024, 2048, 1024
FLOPS = 2 * K * H * S + 2 * 2 * H * N * M

F32 = mybir.dt.float32
BF16 = mybir.dt.bfloat16
I32 = mybir.dt.int32
U32 = mybir.dt.uint32
U16 = mybir.dt.uint16
U8 = mybir.dt.uint8
FP8X4 = mybir.dt.float8_e4m3fn_x4
FP4X4 = mybir.dt.float4_e2m1fn_x4
ALU = mybir.AluOpType
ACT = mybir.ActivationFunctionType

P = 128
PACK = 4
PASS = P * PACK
HALF = 512
LIST_HALF = HALF // 16
STEPS = H // P
F32_MAX = (2.0 - 2.0 ** -23) * 2.0 ** 127


def tile_list_kiln_vent_page_kernel(
    tc, tab_words, tab_scales, offs, w1, smoke0, gain, wgs, page0, offs2, offs3, bar,
    w4_words, w4_scales, w5, wgo, page1, offs4, out,
):
    nc = tc.nc
    with ExitStack() as ctx:
        lists = ctx.enter_context(tc.tile_pool(name="lists", bufs=1))
        keep = ctx.enter_context(tc.tile_pool(name="keep", bufs=1))
        ring = ctx.enter_context(tc.tile_pool(name="ring", bufs=2))
        psum = ctx.enter_context(tc.psum_pool(name="psum", bufs=2))

        def load_list(src, name):
            tile = lists.tile([P, S // 16], U16, name=name)
            nc.sync.dma_start(tile[:], src)
            return tile

        def list_half(tile, half):
            return tile[:, half * LIST_HALF:(half + 1) * LIST_HALF]

        def load_channel_vector(src, name):
            tile = keep.tile([P, STEPS], F32, name=name)
            nc.sync.dma_start(
                tile[:].rearrange("p (a t) -> p a t", t=PACK),
                src.rearrange("(a p t) -> p a t", p=P, t=PACK),
            )
            return tile

        def dealt_rows(src, s):
            a, t = divmod(s, PACK)
            return src[a * PASS:(a + 1) * PASS, :].rearrange("(p t) c -> p t c", t=PACK)[:, t, :]

        def big_tile(shape, name):
            return ring.tile(shape, F32, name=name, tag="big", bufs=6)

        def woven_tile(name, tag="woven", bufs=4):
            return ring.tile([P, PACK * HALF], BF16, name=name, tag=tag, bufs=bufs, align_bytes=64)

        def load_weight(src, kp, cols, name):
            raw = big_tile([P, PACK, HALF], name)
            rows = src[kp * PASS:(kp + 1) * PASS, cols]
            nc.sync.dma_start(raw[:], rows.rearrange("(p j) c -> p j c", j=PACK))
            return raw

        def quantise(woven, codes, scales):
            nc.vector.quantize_mx(out=codes.bitcast(FP8X4), scales=scales, in_=woven[:])

        def mx_tiles(name, width=HALF):
            codes = keep.tile([P, width], U32, name=name + "_codes", align_bytes=64)
            scales = keep.tile([P, width], U8, name=name + "_scales", align_bytes=64)
            return codes, scales

        w1q = {}

        def quantise_w1(a, kp, raw):
            woven = woven_tile("w1_woven")
            copy = nc.vector.tensor_copy if a == 0 else nc.scalar.copy
            copy(
                woven[:].rearrange("p (t m j) -> p m t j", t=PACK, j=PACK),
                raw[:].rearrange("p j (m t) -> p m t j", t=PACK),
            )
            w1q[a, kp] = mx_tiles("w1_%d_%d" % (a, kp))
            quantise(woven, w1q[a, kp][0][:], w1q[a, kp][1][:])

        def weave_w5(a, raw):
            woven = woven_tile("w5_woven", ("g2", "g4")[a], 1)
            nc.scalar.activation(
                woven[:].rearrange("p (c i j) -> p c j i", i=4, j=PACK),
                raw[:].rearrange("p j (c i) -> p c j i", i=4),
                ACT.Copy,
                scale=-1.0,
            )
            return woven

        smoke = {}
        page = {}
        wgs_dealt = {}

        def load_smoke(s, cols=slice(0, S)):
            if s not in smoke:
                smoke[s] = ring.tile([P, S], F32, name="smoke", tag="smoke", bufs=3)
            nc.sync.dma_start(smoke[s][:, cols], dealt_rows(smoke0, s)[:, cols])

        def load_page(s):
            page[s] = big_tile([P, T2], "page")
            nc.sync.dma_start(page[s][:], dealt_rows(page0, s))

        def load_wgs(t, cols=slice(0, S)):
            if t not in wgs_dealt:
                wgs_dealt[t] = ring.tile([P, S], F32, name="wgs", tag="wgs%d" % t, bufs=1, align_bytes=64)
            rows = wgs.rearrange("(m t) j -> m t j", t=PACK)[:, t, cols]
            for q in (0, 2, 1, 3):
                nc.sync.dma_start(wgs_dealt[t][32 * q:32 * (q + 1), cols], rows)

        v_words = {}
        v_scales = {}
        with tc.tile_pool(name="table", bufs=1) as table:
            tab_sc = table.tile([P, T], U8, name="tab_sc")
            nc.vector.memset(tab_sc[:].bitcast(I32), 0)
            def load_words(kp):
                words = table.tile([P, T], I32, name="tab_%d" % kp)
                nc.sync.dma_start(words[:], tab_words[kp].rearrange("p t i -> p (t i)").bitcast(I32))
                return words

            idx = load_list(offs, "idx")
            w1_raw = [load_weight(w1, 0, slice(0, HALF), "w1_raw")]
            gain_sb = load_channel_vector(gain, "gain_sb")
            idx2 = load_list(offs2, "idx2")
            w1_raw.append(load_weight(w1, 1, slice(0, HALF), "w1_raw"))
            bar_sb = load_channel_vector(bar, "bar_sb")
            tab = [load_words(0)]
            idx3 = load_list(offs3, "idx3")
            for q in range(4):
                nc.sync.dma_start(
                    tab_sc[32 * q:32 * q + 8, :].bitcast(I32),
                    tab_scales[:, 4 * q:4 * q + 4, :].bitcast(I32),
                )
            tab.append(load_words(1))
            ident = keep.tile([P, P], F32, name="ident")
            make_identity(nc, ident[:])
            limits = keep.tile([P, 1], F32, name="limits")
            nc.vector.memset(limits[:, 0:1], F32_MAX)
            w4_sc = keep.tile([P, 2, N], U8, name="w4_sc", align_bytes=64)
            nc.vector.memset(w4_sc[:].bitcast(I32), 0)
            load_smoke(0)
            load_wgs(0, slice(0, HALF))
            load_page(0)
            load_wgs(0, slice(HALF, S))
            for kp in range(2):
                quantise_w1(0, kp, w1_raw[kp])
            for half in range(2):
                v_scales[half] = keep.tile([P, HALF], U8, name="v_sc_%d" % half, align_bytes=64)
                nc.vector.tensor_copy(v_scales[half][:], tab_sc[:].indirect(list_half(idx, half)))
                for kp in range(2):
                    v_words[kp, half] = keep.tile([P, HALF], U32, name="v_%d_%d" % (kp, half), align_bytes=64)
                    nc.vector.tensor_copy(
                        v_words[kp, half][:], tab[kp][:].bitcast(U32).indirect(list_half(idx, half))
                    )
        vent = ctx.enter_context(tc.tile_pool(name="vent", bufs=1))

        h = {}

        def make_h(s):
            a, t = divmod(s, PACK)
            h[s] = ring.tile([P, S], F32, name="h", tag="h", bufs=3)
            cols = slice(t * P, (t + 1) * P)
            for half in range(2):
                acc = psum.tile([P, HALF], F32, name="acc")
                for kp in range(2):
                    codes, scales = w1q[a, kp]
                    nc.tensor.matmul_mx(
                        out=acc[:],
                        lhsT=codes[:, cols].bitcast(FP8X4),
                        lhsT_scale=scales[:, cols],
                        rhs=v_words[kp, half][:].bitcast(FP8X4),
                        rhs_scale=v_scales[half][4 * kp:P, :],
                        start=(kp == 0),
                        stop=(kp == 1),
                    )
                if s == 0 and half == 0:
                    diff = ring.tile([P, HALF], F32, name="diff", tag="negated")
                    nc.vector.tensor_tensor(diff[:], acc[:], smoke[s][:, 0:HALF], ALU.subtract)
                    size = ring.tile([P, HALF], F32, name="size", tag="abs_t")
                    nc.vector.scalar_tensor_tensor(size[:], diff[:], -1.0, diff[:], ALU.mult, ALU.max)
                    nc.vector.tensor_scalar(h[s][:, 0:HALF], size[:], gain_sb[:, s:s + 1], None, ALU.mult)
                    continue
                negated = ring.tile([P, HALF], F32, name="negated", tag="negated")
                nc.scalar.activation(negated[:], acc[:], ACT.Copy, scale=-1.0)
                diff_t = psum.tile([P, HALF], F32, name="diff_t")
                blocks = HALF // P
                for b in range(blocks):
                    nc.tensor.matmul(
                        diff_t[:, b * P:(b + 1) * P],
                        smoke[s][:, half * HALF + b * P:half * HALF + (b + 1) * P],
                        ident[:], start=(b == 0), stop=False, is_transpose=True,
                    )
                for b in range(blocks):
                    nc.tensor.matmul(
                        diff_t[:, b * P:(b + 1) * P],
                        negated[:, b * P:(b + 1) * P],
                        ident[:], start=False, stop=(b == blocks - 1), is_transpose=True,
                    )
                abs_t = ring.tile([P, HALF], F32, name="abs_t", tag="abs_t")
                nc.scalar.activation(abs_t[:], diff_t[:], ACT.Abs)
                back = psum.tile([P, HALF], F32, name="back")
                for b in range(blocks):
                    nc.tensor.transpose(back[:, b * P:(b + 1) * P], abs_t[:, b * P:(b + 1) * P], ident[:])
                nc.scalar.activation(
                    h[s][:, half * HALF:(half + 1) * HALF], back[:], ACT.Copy, scale=gain_sb[:, s:s + 1]
                )

        def scatter_page(s):
            if s == 0:
                for half in range(2):
                    cols = slice(half * HALF, (half + 1) * HALF)
                    nc.vector.tensor_tensor(
                        page[s][:].indirect(list_half(idx2, half)), h[s][:, cols], wgs_dealt[0][:, cols], ALU.mult
                    )
            else:
                nc.vector.tensor_tensor(page[s][:].indirect(idx2[:]), h[s][:], wgs_dealt[s % PACK][:], ALU.mult)

        def split_at_bar(s, x, hi_plane, lo_plane):
            nc.vector.tensor_scalar(hi_plane, x, bar_sb[:, s:s + 1], None, ALU.max)
            nc.vector.tensor_scalar(lo_plane, x, bar_sb[:, s:s + 1], None, ALU.min)

        def split_at_bar_beside(s, x, hi_plane, lo_plane):
            nc.gpsimd.tensor_scalar(hi_plane, x, limits[:, 0:1], bar_sb[:, s:s + 1], ALU.min, ALU.max)
            short = ring.tile([P, x.shape[1]], F32, name="short", tag="abs_t")
            nc.scalar.activation(short[:], x, ACT.Relu, bias=bar_sb[:, s:s + 1], scale=-1.0)
            nc.scalar.activation(lo_plane, short[:], ACT.Identity, bias=bar_sb[:, s:s + 1], scale=-1.0)

        def planes_tile(shape, name):
            return ring.tile(shape, BF16, name=name, tag="planes", bufs=3)

        def weave(planes, woven):
            nc.scalar.copy(
                woven[:].rearrange("p (c i t) -> p c t i", i=4, t=PACK),
                planes.rearrange("p t (c i) -> p c t i", i=4),
            )

        def gather_half(s, half, x):
            nc.vector.tensor_copy(x[:], page[s][:].indirect(list_half(idx3, half)))

        def load_second_stage_weights():
            w4 = keep.tile([P, 2, 2 * N], U8, name="w4", align_bytes=64)
            nc.sync.dma_start(w4[:].bitcast(I32), w4_words.rearrange("a p c -> p a c").bitcast(I32))
            for q in range(4):
                nc.sync.dma_start(
                    w4_sc[32 * q:32 * q + 4, :, :].bitcast(I32),
                    w4_scales[:, 4 * q:4 * q + 4, :].rearrange("a r n -> r a n").bitcast(I32),
                )
            return w4

        make_h(0)
        load_smoke(1)
        load_wgs(1)
        load_page(1)
        make_h(1)
        hi0 = planes_tile([P, PACK, M], "hi0")
        lo0 = planes_tile([P, PACK, M], "lo0")
        for s in range(PACK):
            if s == 0:
                load_smoke(2)
                load_wgs(2)
                w1_raw = [load_weight(w1, kp, slice(HALF, 2 * HALF), "w1_raw") for kp in range(2)]
                load_page(2)
            if s == 1:
                load_smoke(3)
                load_wgs(3)
                load_smoke(4)
                load_smoke(5)
                load_smoke(6)
                load_page(3)
                for kp in range(2):
                    quantise_w1(1, kp, w1_raw[kp])
            if s == 2:
                load_smoke(7)
                load_page(4)
            if s == 3:
                load_page(5)
                w5_raw = [load_weight(w5, a, slice(0, N), "w5_raw") for a in range(2)]
            make_h(s + 2)
            scatter_page(s)
            x = ring.tile([P, M], F32, name="x", tag="x", bufs=2)
            nc.vector.tensor_copy(x[:], page[s][:].indirect(idx3[:]))
            split_at_bar_beside(s, x[:], hi0[:, s, :], lo0[:, s, :])

        w4 = load_second_stage_weights()
        idx4 = load_list(offs4, "idx4")
        load_page(6)
        load_page(7)
        wgo_sb = vent.tile([P, M], F32, name="wgo_sb")
        nc.sync.dma_start(wgo_sb[:], wgo)
        vent_page = []
        for n in range(N // P):
            tile = vent.tile([P, T2], F32, name="vent_%d" % n)
            nc.sync.dma_start(tile[:], page1[n * P:(n + 1) * P, :])
            vent_page.append(tile)

        q = {}
        planes = {0: planes_tile([P, 2, PACK, HALF], "planes_0")}
        for s in range(PACK, STEPS):
            t = s - PACK
            if s + 2 < STEPS:
                make_h(s + 2)
            scatter_page(s)
            if s == 7:
                quarters = [ring.tile([P, HALF // 2], F32, name="x", tag=tag, bufs=1) for tag in ("xa", "xb")]
                for i in range(2):
                    offsets = idx3[:, i * LIST_HALF // 2:(i + 1) * LIST_HALF // 2]
                    nc.vector.tensor_copy(quarters[i][:], page[s][:].indirect(offsets))
                for kind, op in enumerate((ALU.max, ALU.min)):
                    for i in range(2):
                        cols = slice(i * HALF // 2, (i + 1) * HALF // 2)
                        nc.vector.tensor_scalar(
                            planes[0][:, kind, t, cols], quarters[i][:], bar_sb[:, s:s + 1], None, op
                        )
            else:
                x = ring.tile([P, HALF], F32, name="x", tag="x", bufs=2)
                gather_half(s, 0, x)
                split_at_bar_beside(s, x[:], planes[0][:, 0, t, :], planes[0][:, 1, t, :])
            if s == 6:
                w5_woven = [weave_w5(a, w5_raw[a]) for a in range(2)]
                w5_codes = ring.tile([P, 2, N], U32, name="w5_codes", tag="wgs2", bufs=1, align_bytes=64)
                w5_scales = keep.tile([P, 2, N], U8, name="w5_scales", align_bytes=64)
                for a in range(2):
                    quantise(w5_woven[a], w5_codes[:, a, :], w5_scales[:, a, :])
            if s in (4, 5):
                kind, src = (("lo", lo0), ("hi", hi0))[s - 4]
                codes = ring.tile([P, M], U32, name="codes0", tag="wgs%d" % t, bufs=1, align_bytes=64)
                scales = keep.tile([P, M], U8, name=kind + "0_scales", align_bytes=64)
                for half in range(2):
                    cols = slice(half * HALF, (half + 1) * HALF)
                    woven = woven_tile("woven")
                    weave(src[:, :, cols], woven)
                    quantise(woven, codes[:, cols], scales[:, cols])
                    q[kind, 0, half] = (codes[:, cols], scales[:, cols])

        def quantise_pass1(half, tags):
            for i, kind in enumerate(("hi", "lo")):
                woven = woven_tile("woven", *tags[i])
                weave(planes[half][:, i, :, :], woven)
                codes, scales = mx_tiles("%s1_%d" % (kind, half))
                quantise(woven, codes[:], scales[:])
                q[kind, 1, half] = (codes[:], scales[:])

        def second_stage(n, half, tag, bufs):
            acc = psum.tile([P, HALF], F32, name="acc2")
            cols = slice(n * P, (n + 1) * P)
            for a in range(2):
                nc.tensor.matmul_mx(
                    out=acc[:],
                    lhsT=w4[:, a, 2 * n * P:2 * (n + 1) * P].bitcast(FP4X4),
                    lhsT_scale=w4_sc[:, a, cols],
                    rhs=q["hi", a, half][0].bitcast(FP8X4),
                    rhs_scale=q["hi", a, half][1],
                    start=(a == 0), stop=False,
                )
                nc.tensor.matmul_mx(
                    out=acc[:],
                    lhsT=w5_codes[:, a, cols].bitcast(FP8X4),
                    lhsT_scale=w5_scales[:, a, cols],
                    rhs=q["lo", a, half][0].bitcast(FP8X4),
                    rhs_scale=q["lo", a, half][1],
                    start=False, stop=(a == 1),
                )
            y = ring.tile([P, HALF], F32, name="y", tag=tag, bufs=bufs, align_bytes=64)
            nc.scalar.copy(y[:], acc[:])
            nc.vector.tensor_tensor(
                vent_page[n][:].indirect(list_half(idx4, half)), y[:],
                wgo_sb[:, half * HALF:(half + 1) * HALF], ALU.mult,
            )

        quantise_pass1(0, (("woven", 4), ("g2", 1)))
        planes[1] = planes_tile([P, 2, PACK, HALF], "planes_1")
        for s, tag in ((4, "xa"), (5, "xb"), (6, "xa"), (7, "g2")):
            if tag != "g2":
                x = ring.tile([P, HALF], F32, name="x", tag=tag, bufs=1)
            else:
                x = ring.tile([P, HALF], F32, name="x", tag=tag, bufs=1, align_bytes=64)
            gather_half(s, 1, x)
            if s < 6:
                nc.gpsimd.tensor_scalar(
                    planes[1][:, 0, s - PACK, :], x[:], limits[:, 0:1], bar_sb[:, s:s + 1], ALU.min, ALU.max
                )
                nc.vector.tensor_scalar(planes[1][:, 1, s - PACK, :], x[:], bar_sb[:, s:s + 1], None, ALU.min)
            else:
                split_at_bar(s, x[:], planes[1][:, 0, s - PACK, :], planes[1][:, 1, s - PACK, :])
        for n in range(3):
            second_stage(n, 0, "y", 2)
        quantise_pass1(1, (("g4", 1), ("woven", 4)))
        second_stage(3, 0, "g4", 1)
        for n in range(N // P):
            second_stage(n, 1, "y", 2)
            nc.sync.dma_start(out[n * P:(n + 1) * P, :], vent_page[n][:])
